import numpy as np
CORES = [2,6,18,22,34,38,50,54,66,70,82,86,98,102,114,118]
N = 16
COUNTS = [[0,1,1,1,1,1,1,1,1,1,4,1,1,1,0,0],[1,0,0,1,0,0,1,0,1,1,4,0,1,1,1,0],[1,1,0,1,0,1,1,0,1,1,4,1,1,1,1,0],[0,0,1,0,1,1,0,1,0,1,4,1,1,0,1,1],[1,1,1,1,0,1,1,1,0,1,4,0,1,0,1,0],[1,0,1,1,1,0,0,1,1,1,4,1,1,0,0,1],[1,1,0,0,1,0,0,0,1,1,4,1,0,1,1,0],[1,0,1,0,1,0,0,0,1,1,4,0,0,1,1,1],[1,1,1,1,1,1,0,1,0,1,4,1,0,1,0,0],[1,1,0,1,1,1,0,1,1,0,4,1,1,1,1,0],[0,1,1,0,0,1,0,1,1,1,0,1,1,1,1,1],[1,1,1,0,1,0,1,0,1,0,4,0,1,0,1,0],[1,1,0,1,1,1,0,1,1,1,4,1,0,1,1,0],[1,1,1,0,0,1,0,1,1,1,4,1,0,0,0,0],[1,0,1,1,0,0,1,0,1,1,4,1,1,0,0,1],[0,0,0,1,0,1,1,1,0,1,4,0,1,1,0,0]]
XW, YW = 16, 60
def setup_inputs(rng):
    return {"x": rng.standard_normal((N, 128, XW), dtype=np.float32)}
def reference(x):
    y = np.full((N, 128, YW), np.nan, x.dtype)
    fill = [0] * N
    for s in range(N):
        o = 0
        for d in range(N):
            c = COUNTS[s][d]
            y[d][:, fill[d]:fill[d] + c] = x[s][:, o:o + c]
            o += c; fill[d] += c
    return {"y": y}

from concourse.bass import DstId, RemoteDMATransfer

SCRATCH = {
    "xs": ("sbuf", [128, 16], "float32"),
    "land": ("sbuf", [128, 60], "float32"),
}
SEMAPHORES = ["loaded", "sent", "arrived", "stored"]


def _bits(m):
    return bin(m).count("1")


def _plan(s, counts, cores, topo):
    n = len(cores)
    by_width = {}
    o = 0
    for d in range(n):
        c = counts[s][d]
        if c:
            f = sum(counts[r][d] for r in range(s))
            by_width.setdefault(c, []).append((d, o, f, c))
        o += c
    calls = []
    for w in sorted(by_width, reverse=True):
        near = [p for p in by_width[w] if topo.chip(cores[p[0]]) == topo.chip(cores[s])]
        far = [p for p in by_width[w] if topo.chip(cores[p[0]]) != topo.chip(cores[s])]
        group = []
        for i in range(0, len(far), 8):
            part = far[i:i + 8]
            e = 8
            while e * len(part) > 8:
                e //= 2
            group.append([p + ((((1 << e) - 1) << (k * e)),) for k, p in enumerate(part)])
        if near:
            if not group:
                group.append([])
            group[0].extend(p + (0xFF00,) for p in near)
        calls.extend(group)
    return calls


def rank_program(g, core, T, topo):
    me = T.rank_of(core)
    if me is None:
        return
    counts = T.tables["COUNTS"]
    cores = list(T.cores)
    n = len(cores)

    g.sync.dma_start(T.xs[:], T.x[:]).then_inc(T.sem.loaded, 16)
    g.wait_ge(T.sem.loaded, 16)

    sent = 0
    for call in _plan(me, counts, cores, topo):
        transfers = []
        for d, o, f, c, m in call:
            rid, pid, _se = topo.addr(cores[d])
            transfers.append(RemoteDMATransfer(
                dst_ids=[DstId(rid=rid, pnc=pid)], dma_engine_mask=m, remote_sem=T.sem.arrived,
                src=T.xs[:, o:o + c], dst=T.land[:, f:f + c]))
            sent += _bits(m)
        g.remote_dma_fused(transfers, local_sem=T.sem.sent)

    due = sum(_bits(p[4]) for s in range(n) if s != me
              for call in _plan(s, counts, cores, topo) for p in call if p[0] == me)
    total = sum(counts[s][me] for s in range(n))
    if due:
        g.sync.wait_ge(T.sem.arrived, due)
        g.sync.dma_start(T.y[:, 0:total], T.land[:, 0:total]).then_inc(T.sem.stored, 16)
        g.sync.wait_ge(T.sem.stored, 16)
    if sent:
        g.wait_ge(T.sem.sent, sent)
